import numpy as np
import ml_dtypes


def mxq(x, axis, fmt="e4m3"):
    dtype, down = {"e4m3": (ml_dtypes.float8_e4m3fn, 7), "e5m2": (ml_dtypes.float8_e5m2, 14)}[fmt]
    v = np.moveaxis(np.asarray(x, np.float32).astype(ml_dtypes.bfloat16).astype(np.float64), axis, -1)
    blocks = v.reshape(v.shape[:-1] + (-1, 32))
    amax = np.abs(blocks).max(-1, keepdims=True)
    byte = np.maximum(np.where(amax > 0, np.frexp(amax)[1] - 1 + 127, 0) - down, 1)
    scale = np.exp2(byte - 127.0)
    codes = (blocks / scale).astype(np.float32).astype(dtype).astype(np.float64)
    return np.moveaxis((codes * scale).reshape(v.shape), -1, axis)


WIDE = False


def mx_kscale(k):
    if not WIDE:
        return np.ones(k)
    levels = np.array([10, -10, 5, -5, 0])
    if k % 512:
        return np.exp2(np.random.permutation(np.resize(levels, k // 32))).repeat(32)
    a = np.empty((k // 512, 16))
    for p in range(k // 512):
        a[p, :8] = np.random.permutation(np.resize(levels, 8))
        for g in range(8):
            far = levels[np.abs(levels - a[p, g]) >= 10]
            a[p, g + 8] = far[np.random.randint(len(far))]
    return np.exp2(a.ravel()).repeat(32)


def f64(x):
    return np.asarray(x).astype(np.float64)


def striped(idx):
    return np.tile(idx.reshape(-1, 16).T, (8, 1)).astype(np.uint16)


def unstriped(offs):
    return offs[:16].T.reshape(-1).astype(np.int64)


E2M1 = np.array([0.0, 0.5, 1.0, 1.5, 2.0, 3.0, 4.0, 6.0, -0.0, -0.5, -1.0, -1.5, -2.0, -3.0, -4.0, -6.0])


def pack_weight(w, fmt):
    k, n = w.shape
    w = f64(np.asarray(w, np.float32).astype(ml_dtypes.bfloat16)).reshape(k // 32, 32, n)
    amax = np.abs(w).max(1)
    if fmt == "e4m3":
        byte = np.frexp(amax)[1] - 1 + 127 - 7
    else:
        mant, ex = np.frexp(amax / 6.0)
        byte = np.where(mant > 0.5, ex, ex - 1) + 127
    byte = np.clip(np.where(amax > 0, byte, 1), 1, 254)
    scaled = (w * np.exp2(127.0 - byte)[:, None, :]).reshape(k, n).astype(np.float32)
    by_word = np.ascontiguousarray(scaled.reshape(k // 512, 128, 4, n).transpose(0, 1, 3, 2))
    if fmt == "e4m3":
        words = by_word.astype(ml_dtypes.float8_e4m3fn).view(np.uint8)
    else:
        c = by_word.astype(ml_dtypes.float4_e2m1fn).view(np.uint8) & 0xF
        words = (c[..., 0::2] | (c[..., 1::2] << 4)).reshape(k // 512, 128, 2 * n)
    return np.ascontiguousarray(words), np.ascontiguousarray(byte.astype(np.uint8).reshape(k // 512, 16, n))


def unpack_weight(words, scales, fmt):
    g, _, n = scales.shape
    words = np.ascontiguousarray(words).reshape(g, 128, n, -1)
    if fmt == "e4m3":
        vals = words.view(ml_dtypes.float8_e4m3fn).astype(np.float64)
    else:
        nib = np.empty((g, 128, n, 4), np.uint8)
        nib[..., 0::2] = words & 0xF
        nib[..., 1::2] = words >> 4
        vals = E2M1[nib]
    vals = vals * np.repeat(np.exp2(scales.astype(np.float64) - 127.0), 8, axis=1)[..., None]
    return vals.transpose(0, 1, 3, 2).reshape(g * 512, n)


def gelu(v):
    return 0.5 * v * (1.0 + np.tanh(np.sqrt(2.0 / np.pi) * (v + 0.044715 * v**3)))


def striped8(idx):
    return np.concatenate([v.reshape(-1, 16).T for v in idx]).astype(np.uint16)


def unstriped8(offs):
    return np.stack([offs[16 * g:16 * g + 16].T.reshape(-1) for g in range(8)]).astype(np.int64)


def heads(h, wgt, idx8):
    r = np.arange(h.shape[0])
    return wgt[r // 4 % 128] * h[r[:, None], idx8[r % 512 // 64]]


K, H, N, T, S, T2, P = 1536, 1024, 768, 4096, 1024, 2048, 1024

def setup_inputs():
    n = np.random.standard_normal
    s = mx_kscale(K)[:, None]
    u = mx_kscale(H)[:, None]
    tab_words, tab_scales = pack_weight(n((K, T)) * s, "e4m3")
    w2_words, w2_scales = pack_weight(1.5 * n((H, N)) / np.sqrt(H) / u, "e2m1")
    return {
        "tab_words": tab_words, "tab_scales": tab_scales,
        "offs": striped(np.random.permutation(T)[:S]),
        "w1": (1.5 * n((K, H)) / np.sqrt(K) / s).astype(np.float32),
        "b1": (0.7 * n(H)).astype(np.float32),
        "motion": (n((H, S)) * u).astype(np.float32),
        "page0": (n((H, T2)) * u).astype(np.float32),
        "wgs": np.exp(0.3 * n((128, S))).astype(np.float32),
        "offs2": striped(np.random.permutation(T2)[:S]),
        "wgt": np.repeat(np.random.uniform(0.5, 2.0, (8, P)), 16, axis=0).astype(np.float32),
        "offs3": striped8(np.stack([np.random.permutation(T2)[:P] for _ in range(8)])),
        "w2_words": w2_words, "w2_scales": w2_scales,
        "vis": np.exp(0.4 * n((N, P))).astype(np.float32),
    }

def reference(tab_words, tab_scales, offs, w1, b1, motion, page0, wgs, offs2, wgt, offs3, w2_words, w2_scales, vis):
    v = unpack_weight(tab_words, tab_scales, "e4m3")[:, unstriped(offs)]
    w1q = mxq(f64(w1), 0, "e4m3")
    h = np.tanh((w1q.T @ v) + f64(b1)[:, None]) * f64(motion)
    page = f64(page0).copy()
    page[:, unstriped(offs2)] = np.tile(f64(wgs), (H // 128, 1)) * h
    x = heads(page, f64(wgt), unstriped8(offs3))
    xq = mxq(x, 0, "e4m3")
    w2 = unpack_weight(w2_words, w2_scales, "e2m1")
    y = np.tanh(w2.T @ xq)
    return y * f64(vis)

@@ -1,0 +1,267 @@
+from contextlib import ExitStack
+
+import concourse.mybir as mybir
+
+K, H, N, T, S, T2, M = 1536, 1024, 768, 4096, 1024, 2048, 1024
+FLOPS = 2 * K * H * S + 2 * H * N * M
+
+F32 = mybir.dt.float32
+BF16 = mybir.dt.bfloat16
+I32 = mybir.dt.int32
+U32 = mybir.dt.uint32
+U16 = mybir.dt.uint16
+U8 = mybir.dt.uint8
+FP8X4 = mybir.dt.float8_e4m3fn_x4
+FP4X4 = mybir.dt.float4_e2m1fn_x4
+MULT = mybir.AluOpType.mult
+TANH = mybir.ActivationFunctionType.Tanh
+
+P = 128
+PACK = 4
+PASS = P * PACK
+BANK = 512
+K_PASSES = K // PASS
+R_PASSES = H // PASS
+SLICES = R_PASSES * PACK
+LIST_COLS = 16
+CUES = 256
+KB = 1024
+
+
+def tile_list_approach_cue_scores_kernel(
+    tc, tab_words, tab_scales, offs, w1, b1, motion, page0, wgs, offs2, wgt, offs3, w2_words, w2_scales, vis, out
+):
+    nc = tc.nc
+    with ExitStack() as ctx:
+        keep = ctx.enter_context(tc.tile_pool(name="keep", bufs=1))
+        arena = ctx.enter_context(tc.tile_pool(name="arena", bufs=1))
+        psum = ctx.enter_context(tc.psum_pool(name="psum", bufs=4))
+
+        def held(name, shape, dtype):
+            return keep.tile(shape, dtype, name=name, align_bytes=64)
+
+        def placed(name, shape, dtype, kib):
+            return arena.tile(shape, dtype, name=name, align_bytes=64, offset=kib * KB)
+
+        TABLE_AT, PAGES_AT, RAW_AT, ROUND_AT, MOTION_AT, H_AT, WGS_AT = 0, 48, 80, 104, 120, 136, 152
+
+        list1 = held("list1", [P, S // LIST_COLS], U16)
+        list2 = held("list2", [P, S // LIST_COLS], U16)
+        list3 = held("list3", [P, M // LIST_COLS], U16)
+        tab_planes = held("tab_planes", [P, T], U8)
+        v_planes = held("v_planes", [P, S], U8)
+        v_words = [held(f"v_words{a}", [P, S], U32) for a in range(K_PASSES)]
+        w1_words = [[held(f"w1_words{b}_{a}", [P, PASS], U32) for a in range(K_PASSES)] for b in range(R_PASSES)]
+        w1_plane = [[held(f"w1_plane{b}_{a}", [P, PASS], U8) for a in range(K_PASSES)] for b in range(R_PASSES)]
+        bias = held("bias", [P, R_PASSES, PACK], F32)
+        wgt_sb = held("wgt_sb", [P, M], F32)
+        w2_codes = held("w2_codes", [P, R_PASSES, 2 * N], U8)
+        w2_plane = held("w2_plane", [P, R_PASSES, N], U8)
+        x_words = [held(f"x_words{b}", [P, M], U32) for b in range(R_PASSES)]
+        x_plane = [held(f"x_plane{b}", [P, M], U8) for b in range(R_PASSES)]
+
+        motion_rows = motion.rearrange("(b p t) j -> b t p j", b=R_PASSES, t=PACK)
+        page_rows = page0.rearrange("(b p t) c -> b t p c", b=R_PASSES, t=PACK)
+        wgs_rows = wgs.rearrange("(q t) j -> q t j", t=PACK)
+        out_rows = out.rearrange("(i p) m -> p i m", p=P)
+        vis_rows = vis.rearrange("(i p) m -> p i m", p=P)
+
+        nc.gpsimd.memset(tab_planes[:].bitcast(U32), 0)
+        for q in range(4):
+            nc.gpsimd.dma_start(
+                out=tab_planes[32 * q : 32 * q + 4 * K_PASSES, :].bitcast(I32),
+                in_=tab_scales[:, 4 * q : 4 * q + 4, :].bitcast(I32),
+            )
+        nc.scalar.dma_start(out=bias[:], in_=b1.rearrange("(b p t) -> p b t", b=R_PASSES, t=PACK))
+        nc.gpsimd.memset(w2_plane[:].rearrange("p a c -> p (a c)").bitcast(U32), 0)
+        for q in range(4):
+            nc.gpsimd.dma_start(
+                out=w2_plane[32 * q : 32 * q + 4, :, :].bitcast(I32),
+                in_=w2_scales[:, 4 * q : 4 * q + 4, :].rearrange("a r c -> r a c").bitcast(I32),
+            )
+
+        def load_w1(b, a):
+            raw = placed(f"w1_raw{b}_{a}", [P, PACK, PASS], F32, RAW_AT + 8 * a)
+            rows = w1[a * PASS : (a + 1) * PASS, b * PASS : (b + 1) * PASS]
+            nc.sync.dma_start(out=raw[:], in_=rows.rearrange("(p i) c -> p i c", i=PACK))
+            return raw
+
+        def round_w1(b, a, raw):
+            rounded = placed(f"w1_round{b}_{a}", [P, PACK, P, PACK], BF16, ROUND_AT + 4 * ((b * K_PASSES + a) % 2))
+            nc.scalar.copy(
+                out=rounded[:].rearrange("p t q i -> p q i t"),
+                in_=raw[:].rearrange("p i (q t) -> p q i t", t=PACK),
+            )
+            return rounded
+
+        def quantise_w1(b, a, rounded):
+            nc.vector.quantize_mx(
+                out=w1_words[b][a][:].bitcast(FP8X4),
+                scales=w1_plane[b][a][:],
+                in_=rounded[:].rearrange("p t q i -> p (t q i)"),
+            )
+
+        def load_table(a):
+            words = placed(f"tab{a}", [P, T], I32, TABLE_AT + 16 * a)
+            nc.sync.dma_start(out=words[:], in_=tab_words[a].rearrange("p t i -> p (t i)").bitcast(I32))
+            return words
+
+        def load_motion(s):
+            tile = placed(f"motion{s}", [P, S], F32, MOTION_AT + 4 * (s % 4))
+            nc.sync.dma_start(out=tile[:], in_=motion_rows[s // PACK, s % PACK])
+            return tile
+
+        def load_page(s):
+            at = PAGES_AT + 8 * s if s < PACK else TABLE_AT + 8 * (s - PACK)
+            tile = placed(f"page{s}", [P, T2], F32, at)
+            nc.sync.dma_start(out=tile[:], in_=page_rows[s // PACK, s % PACK])
+            return tile
+
+        nc.sync.dma_start(list1[:], offs)
+        for a in range(K_PASSES):
+            raw = load_w1(0, a)
+            words = load_table(a)
+            quantise_w1(0, a, round_w1(0, a, raw))
+            if a == 0:
+                nc.vector.tensor_copy(v_planes[:], tab_planes[:].indirect(list1[:]))
+            if a < K_PASSES - 1:
+                nc.vector.tensor_copy(v_words[a][:], words[:].bitcast(U32).indirect(list1[:]))
+            else:
+                for half in range(S // BANK):
+                    cols = slice(half * BANK, (half + 1) * BANK)
+                    part = list1[:, half * BANK // LIST_COLS : (half + 1) * BANK // LIST_COLS]
+                    nc.vector.tensor_copy(v_words[a][:, cols], words[:].bitcast(U32).indirect(part))
+
+        motions = {0: load_motion(0)}
+        wgs_first = placed("wgs_first", [P, S], F32, WGS_AT)
+        wgs_rest = placed("wgs_rest", [P, PACK - 1, S], F32, WGS_AT + 4)
+        for q in range(4):
+            nc.sync.dma_start(out=wgs_first[32 * q : 32 * q + 32, :], in_=wgs_rows[:, 0, :])
+        nc.sync.dma_start(list2[:], offs2)
+        pages = {0: load_page(0)}
+        motions[1] = load_motion(1)
+        for q in range(4):
+            nc.sync.dma_start(out=wgs_rest[32 * q : 32 * q + 32, :, :], in_=wgs_rows[:, 1:, :])
+        wgs_of = [wgs_first[:]] + [wgs_rest[:, t, :] for t in range(PACK - 1)]
+        pages[1] = load_page(1)
+        nc.sync.dma_start(list3[:], offs3)
+        nc.sync.dma_start(out=wgt_sb[:], in_=wgt)
+        for s in range(2, PACK):
+            motions[s] = load_motion(s)
+            pages[s] = load_page(s)
+        raws = [load_w1(1, a) for a in range(K_PASSES)]
+
+        def features(s):
+            b, t = divmod(s, PACK)
+            h = placed(f"h{s}", [P, S], F32, H_AT + 4 * (s % 4))
+            for half in range(S // BANK):
+                cols = slice(half * BANK, (half + 1) * BANK)
+                acc = psum.tile([P, BANK], F32, name="acc1")
+                for a in range(K_PASSES):
+                    nc.tensor.matmul_mx(
+                        out=acc[:],
+                        lhsT=w1_words[b][a][:, t * P : (t + 1) * P].bitcast(FP8X4),
+                        lhsT_scale=w1_plane[b][a][:, t * P : (t + 1) * P],
+                        rhs=v_words[a][:, cols].bitcast(FP8X4),
+                        rhs_scale=v_planes[4 * a : P, cols],
+                        start=(a == 0),
+                        stop=(a == K_PASSES - 1),
+                    )
+                nc.scalar.activation(out=h[:, cols], in_=acc[:], func=TANH, bias=bias[:, b, t : t + 1])
+            return h
+
+        def times_motion(s, h, cols):
+            nc.vector.tensor_tensor(h[:, cols], h[:, cols], motions[s][:, cols], MULT)
+
+        def put(s, h, cols):
+            part = list2[:, cols.start // LIST_COLS : cols.stop // LIST_COLS]
+            nc.vector.tensor_tensor(pages[s][:].indirect(part), h[:, cols], wgs_of[s % PACK][:, cols], MULT)
+
+        def pick(s, picked, cols):
+            part = list3[:, cols.start // LIST_COLS : cols.stop // LIST_COLS]
+            nc.vector.tensor_tensor(picked[:, s % PACK, :], pages[s][:].indirect(part), wgt_sb[:, cols], MULT)
+
+        def round_x(name, picked, width, kib):
+            rounded = placed(name, [P, width, PACK], BF16, kib)
+            nc.scalar.copy(
+                out=rounded[:].rearrange("p (c e) t -> p c t e", e=4),
+                in_=picked[:].rearrange("p t (c e) -> p c t e", e=4),
+            )
+            return rounded
+
+        def quantise_x(b, rounded, cols):
+            nc.vector.quantize_mx(
+                out=x_words[b][:, cols].bitcast(FP8X4),
+                scales=x_plane[b][:, cols],
+                in_=rounded[:].rearrange("p m t -> p (m t)"),
+            )
+
+        whole = slice(0, S)
+        picked0 = placed("picked0", [P, PACK, M], F32, TABLE_AT + 32)
+        hs = {}
+        for s in range(SLICES):
+            if s == PACK - 1:
+                for a in range(K_PASSES):
+                    quantise_w1(1, a, round_w1(1, a, raws[a]))
+                for later in range(PACK, SLICES):
+                    motions[later] = load_motion(later)
+                    pages[later] = load_page(later)
+                nc.sync.dma_start(
+                    out=w2_codes[:].bitcast(I32), in_=w2_words.rearrange("a p c -> p a c").bitcast(I32)
+                )
+                vis_sb = []
+                for pair in range(N // (2 * P)):
+                    tile = placed(f"vis{pair}", [P, 2, M], F32, RAW_AT + 8 * pair)
+                    nc.sync.dma_start(out=tile[:], in_=vis_rows[:, 2 * pair : 2 * pair + 2, :])
+                    vis_sb.append(tile)
+            hs[s] = features(s)
+            if s == 0:
+                for half in range(S // BANK):
+                    cols = slice(half * BANK, (half + 1) * BANK)
+                    times_motion(s, hs[s], cols)
+                    put(s, hs[s], cols)
+            else:
+                times_motion(s, hs[s], whole)
+                put(s, hs[s], whole)
+            if 1 <= s <= PACK:
+                pick(s - 1, picked0, whole)
+            if s == PACK:
+                quantise_x(0, round_x("x_round0", picked0, M, ROUND_AT + 8), whole)
+
+        chunks = M // CUES
+        picked_at = [TABLE_AT + 32, TABLE_AT + 36, H_AT + 12, WGS_AT + 12]
+
+        def pick_chunk(c):
+            cols = slice(c * CUES, (c + 1) * CUES)
+            picked = placed(f"picked1_{c}", [P, PACK, CUES], F32, picked_at[c])
+            for s in range(PACK, SLICES):
+                pick(s, picked, cols)
+            return round_x(f"x_round1_{c}", picked, CUES, ROUND_AT + 2 * c)
+
+        def scores(c, rounded):
+            cols = slice(c * CUES, (c + 1) * CUES)
+            quantise_x(1, rounded, cols)
+            for pair in range(N // (2 * P)):
+                acc = psum.tile([P, 2, CUES], F32, name="acc2")
+                for u in range(2):
+                    i = 2 * pair + u
+                    for b in range(R_PASSES):
+                        nc.tensor.matmul_mx(
+                            out=acc[:, u, :],
+                            lhsT=w2_codes[:, b, 2 * P * i : 2 * P * (i + 1)].bitcast(FP4X4),
+                            lhsT_scale=w2_plane[:, b, P * i : P * (i + 1)],
+                            rhs=x_words[b][:, cols].bitcast(FP8X4),
+                            rhs_scale=x_plane[b][:, cols],
+                            start=(b == 0),
+                            stop=(b == R_PASSES - 1),
+                        )
+                y = placed(f"y{c}_{pair}", [P, 2, CUES], F32, PAGES_AT + 2 * (3 * c + pair))
+                nc.scalar.activation(out=y[:], in_=acc[:], func=TANH)
+                nc.vector.tensor_tensor(y[:], y[:], vis_sb[pair][:, :, cols], MULT)
+                nc.sync.dma_start(out=out_rows[:, 2 * pair : 2 * pair + 2, cols], in_=y[:])
+
+        rounded = {0: pick_chunk(0)}
+        for c in range(chunks):
+            if c + 1 < chunks:
+                rounded[c + 1] = pick_chunk(c + 1)
+            scores(c, rounded[c])

@@ -43,13 +43,12 @@ def tile_list_approach_cue_scores_kernel(
         def placed(name, shape, dtype, kib):
             return arena.tile(shape, dtype, name=name, align_bytes=64, offset=kib * KB)
 
-        TABLE_AT, PAGES_AT, RAW_AT, ROUND_AT, MOTION_AT, H_AT, WGS_AT = 0, 48, 80, 104, 120, 136, 152
+        TABLE_AT, PAGES_AT, RAW_AT, ROUND_AT, MOTION_AT, H_AT, WGS_AT = 0, 49, 81, 105, 121, 137, 153
 
         list1 = held("list1", [P, S // LIST_COLS], U16)
         list2 = held("list2", [P, S // LIST_COLS], U16)
         list3 = held("list3", [P, M // LIST_COLS], U16)
         tab_planes = held("tab_planes", [P, T], U8)
-        v_planes = held("v_planes", [P, S], U8)
         v_words = [held(f"v_words{a}", [P, S], U32) for a in range(K_PASSES)]
         w1_words = [[held(f"w1_words{b}_{a}", [P, PASS], U32) for a in range(K_PASSES)] for b in range(R_PASSES)]
         w1_plane = [[held(f"w1_plane{b}_{a}", [P, PASS], U8) for a in range(K_PASSES)] for b in range(R_PASSES)]
@@ -66,19 +65,14 @@ def tile_list_approach_cue_scores_kernel(
         out_rows = out.rearrange("(i p) m -> p i m", p=P)
         vis_rows = vis.rearrange("(i p) m -> p i m", p=P)
 
-        nc.gpsimd.memset(tab_planes[:].bitcast(U32), 0)
+        nc.vector.memset(tab_planes[:].bitcast(U32), 0)
         for q in range(4):
-            nc.gpsimd.dma_start(
+            nc.scalar.dma_start(
                 out=tab_planes[32 * q : 32 * q + 4 * K_PASSES, :].bitcast(I32),
                 in_=tab_scales[:, 4 * q : 4 * q + 4, :].bitcast(I32),
             )
         nc.scalar.dma_start(out=bias[:], in_=b1.rearrange("(b p t) -> p b t", b=R_PASSES, t=PACK))
-        nc.gpsimd.memset(w2_plane[:].rearrange("p a c -> p (a c)").bitcast(U32), 0)
-        for q in range(4):
-            nc.gpsimd.dma_start(
-                out=w2_plane[32 * q : 32 * q + 4, :, :].bitcast(I32),
-                in_=w2_scales[:, 4 * q : 4 * q + 4, :].rearrange("a r c -> r a c").bitcast(I32),
-            )
+        nc.vector.memset(w2_plane[:].rearrange("p a c -> p (a c)").bitcast(U32), 0)
 
         def load_w1(b, a):
             raw = placed(f"w1_raw{b}_{a}", [P, PACK, PASS], F32, RAW_AT + 8 * a)
@@ -102,7 +96,7 @@ def tile_list_approach_cue_scores_kernel(
             )
 
         def load_table(a):
-            words = placed(f"tab{a}", [P, T], I32, TABLE_AT + 16 * a)
+            words = placed(f"tab{a}", [P, T], I32, TABLE_AT + (16, 0, 32)[a])
             nc.sync.dma_start(out=words[:], in_=tab_words[a].rearrange("p t i -> p (t i)").bitcast(I32))
             return words
 
@@ -112,7 +106,7 @@ def tile_list_approach_cue_scores_kernel(
             return tile
 
         def load_page(s):
-            at = PAGES_AT + 8 * s if s < PACK else TABLE_AT + 8 * (s - PACK)
+            at = PAGES_AT + 8 * s if s < PACK else TABLE_AT + 1 + 8 * (s - PACK)
             tile = placed(f"page{s}", [P, T2], F32, at)
             nc.sync.dma_start(out=tile[:], in_=page_rows[s // PACK, s % PACK])
             return tile
@@ -122,38 +116,37 @@ def tile_list_approach_cue_scores_kernel(
             raw = load_w1(0, a)
             words = load_table(a)
             quantise_w1(0, a, round_w1(0, a, raw))
-            if a == 0:
-                nc.vector.tensor_copy(v_planes[:], tab_planes[:].indirect(list1[:]))
             if a < K_PASSES - 1:
                 nc.vector.tensor_copy(v_words[a][:], words[:].bitcast(U32).indirect(list1[:]))
+                if a == 1:
+                    v_planes = placed("v_planes", [P, S], U8, TABLE_AT)
+                    nc.vector.tensor_copy(v_planes[:], tab_planes[:].indirect(list1[:]))
             else:
                 for half in range(S // BANK):
                     cols = slice(half * BANK, (half + 1) * BANK)
                     part = list1[:, half * BANK // LIST_COLS : (half + 1) * BANK // LIST_COLS]
                     nc.vector.tensor_copy(v_words[a][:, cols], words[:].bitcast(U32).indirect(part))
 
-        motions = {0: load_motion(0)}
-        wgs_first = placed("wgs_first", [P, S], F32, WGS_AT)
-        wgs_rest = placed("wgs_rest", [P, PACK - 1, S], F32, WGS_AT + 4)
-        for q in range(4):
-            nc.sync.dma_start(out=wgs_first[32 * q : 32 * q + 32, :], in_=wgs_rows[:, 0, :])
+        def load_wgs(t):
+            tile = placed(f"wgs{t}", [P, S], F32, WGS_AT + 4 * t)
+            for q in range(4):
+                nc.sync.dma_start(out=tile[32 * q : 32 * q + 32, :], in_=wgs_rows[:, t, :])
+            return tile
+
+        motions, wgs_of, pages, raws = {}, {}, {}, {}
+        motions[0], wgs_of[0] = load_motion(0), load_wgs(0)
         nc.sync.dma_start(list2[:], offs2)
-        pages = {0: load_page(0)}
-        motions[1] = load_motion(1)
-        for q in range(4):
-            nc.sync.dma_start(out=wgs_rest[32 * q : 32 * q + 32, :, :], in_=wgs_rows[:, 1:, :])
-        wgs_of = [wgs_first[:]] + [wgs_rest[:, t, :] for t in range(PACK - 1)]
-        pages[1] = load_page(1)
+        pages[0] = load_page(0)
+        motions[1], wgs_of[1], pages[1] = load_motion(1), load_wgs(1), load_page(1)
+        motions[2], wgs_of[2], raws[0], pages[2] = load_motion(2), load_wgs(2), load_w1(1, 0), load_page(2)
+        raws[1], motions[3], wgs_of[3], raws[2] = load_w1(1, 1), load_motion(3), load_wgs(3), load_w1(1, 2)
         nc.sync.dma_start(list3[:], offs3)
         nc.sync.dma_start(out=wgt_sb[:], in_=wgt)
-        for s in range(2, PACK):
-            motions[s] = load_motion(s)
-            pages[s] = load_page(s)
-        raws = [load_w1(1, a) for a in range(K_PASSES)]
+        pages[3] = load_page(3)
 
         def features(s):
             b, t = divmod(s, PACK)
-            h = placed(f"h{s}", [P, S], F32, H_AT + 4 * (s % 4))
+            h = placed(f"h{s}", [P, S], F32, TABLE_AT + 33 if s == 5 else H_AT + 4 * (s % 4))
             for half in range(S // BANK):
                 cols = slice(half * BANK, (half + 1) * BANK)
                 acc = psum.tile([P, BANK], F32, name="acc1")
@@ -170,12 +163,13 @@ def tile_list_approach_cue_scores_kernel(
                 nc.scalar.activation(out=h[:, cols], in_=acc[:], func=TANH, bias=bias[:, b, t : t + 1])
             return h
 
-        def times_motion(s, h, cols):
-            nc.vector.tensor_tensor(h[:, cols], h[:, cols], motions[s][:, cols], MULT)
+        def times_factors(engine, s, h, cols):
+            engine.tensor_tensor(h[:, cols], h[:, cols], motions[s][:, cols], MULT)
+            engine.tensor_tensor(h[:, cols], h[:, cols], wgs_of[s % PACK][:, cols], MULT)
 
         def put(s, h, cols):
             part = list2[:, cols.start // LIST_COLS : cols.stop // LIST_COLS]
-            nc.vector.tensor_tensor(pages[s][:].indirect(part), h[:, cols], wgs_of[s % PACK][:, cols], MULT)
+            nc.vector.tensor_copy(pages[s][:].indirect(part), h[:, cols])
 
         def pick(s, picked, cols):
             part = list3[:, cols.start // LIST_COLS : cols.stop // LIST_COLS]
@@ -197,7 +191,6 @@ def tile_list_approach_cue_scores_kernel(
             )
 
         whole = slice(0, S)
-        picked0 = placed("picked0", [P, PACK, M], F32, TABLE_AT + 32)
         hs = {}
         for s in range(SLICES):
             if s == PACK - 1:
@@ -209,6 +202,11 @@ def tile_list_approach_cue_scores_kernel(
                 nc.sync.dma_start(
                     out=w2_codes[:].bitcast(I32), in_=w2_words.rearrange("a p c -> p a c").bitcast(I32)
                 )
+                for q in range(4):
+                    nc.sync.dma_start(
+                        out=w2_plane[32 * q : 32 * q + 4, :, :].bitcast(I32),
+                        in_=w2_scales[:, 4 * q : 4 * q + 4, :].rearrange("a r c -> r a c").bitcast(I32),
+                    )
                 vis_sb = []
                 for pair in range(N // (2 * P)):
                     tile = placed(f"vis{pair}", [P, 2, M], F32, RAW_AT + 8 * pair)
@@ -218,29 +216,30 @@ def tile_list_approach_cue_scores_kernel(
             if s == 0:
                 for half in range(S // BANK):
                     cols = slice(half * BANK, (half + 1) * BANK)
-                    times_motion(s, hs[s], cols)
+                    times_factors(nc.vector, s, hs[s], cols)
                     put(s, hs[s], cols)
             else:
-                times_motion(s, hs[s], whole)
+                times_factors(nc.gpsimd, s, hs[s], whole)
                 put(s, hs[s], whole)
-            if 1 <= s <= PACK:
-                pick(s - 1, picked0, whole)
-            if s == PACK:
+            if s == 5:
+                picked0 = placed("picked0", [P, PACK, M], F32, TABLE_AT + 33)
+                for early in range(PACK):
+                    pick(early, picked0, whole)
                 quantise_x(0, round_x("x_round0", picked0, M, ROUND_AT + 8), whole)
 
         chunks = M // CUES
-        picked_at = [TABLE_AT + 32, TABLE_AT + 36, H_AT + 12, WGS_AT + 12]
+        picked_at = [TABLE_AT + 33, H_AT + 12, ROUND_AT, ROUND_AT + 4]
+        round_at = [ROUND_AT, ROUND_AT + 4, ROUND_AT + 8, ROUND_AT + 10]
 
         def pick_chunk(c):
             cols = slice(c * CUES, (c + 1) * CUES)
             picked = placed(f"picked1_{c}", [P, PACK, CUES], F32, picked_at[c])
             for s in range(PACK, SLICES):
                 pick(s, picked, cols)
-            return round_x(f"x_round1_{c}", picked, CUES, ROUND_AT + 2 * c)
+            return round_x(f"x_round1_{c}", picked, CUES, round_at[c])
 
-        def scores(c, rounded):
+        def scores(c):
             cols = slice(c * CUES, (c + 1) * CUES)
-            quantise_x(1, rounded, cols)
             for pair in range(N // (2 * P)):
                 acc = psum.tile([P, 2, CUES], F32, name="acc2")
                 for u in range(2):
@@ -264,4 +263,6 @@ def tile_list_approach_cue_scores_kernel(
         for c in range(chunks):
             if c + 1 < chunks:
                 rounded[c + 1] = pick_chunk(c + 1)
-            scores(c, rounded[c])
+            quantise_x(1, rounded[c], slice(c * CUES, (c + 1) * CUES))
+        for c in range(chunks):
+            scores(c)

@@ -65,9 +65,9 @@ def tile_list_approach_cue_scores_kernel(
         out_rows = out.rearrange("(i p) m -> p i m", p=P)
         vis_rows = vis.rearrange("(i p) m -> p i m", p=P)
 
-        nc.vector.memset(tab_planes[:].bitcast(U32), 0)
+        nc.gpsimd.memset(tab_planes[:].bitcast(U32), 0)
         for q in range(4):
-            nc.scalar.dma_start(
+            nc.gpsimd.dma_start(
                 out=tab_planes[32 * q : 32 * q + 4 * K_PASSES, :].bitcast(I32),
                 in_=tab_scales[:, 4 * q : 4 * q + 4, :].bitcast(I32),
             )
@@ -83,8 +83,8 @@ def tile_list_approach_cue_scores_kernel(
         def round_w1(b, a, raw):
             rounded = placed(f"w1_round{b}_{a}", [P, PACK, P, PACK], BF16, ROUND_AT + 4 * ((b * K_PASSES + a) % 2))
             nc.scalar.copy(
-                out=rounded[:].rearrange("p t q i -> p q i t"),
-                in_=raw[:].rearrange("p i (q t) -> p q i t", t=PACK),
+                out=rounded[:].rearrange("p t q i -> p q t i"),
+                in_=raw[:].rearrange("p i (q t) -> p q t i", t=PACK),
             )
             return rounded
 
@@ -96,7 +96,7 @@ def tile_list_approach_cue_scores_kernel(
             )
 
         def load_table(a):
-            words = placed(f"tab{a}", [P, T], I32, TABLE_AT + (16, 0, 32)[a])
+            words = placed(f"tab{a}", [P, T], I32, TABLE_AT + 16 * a)
             nc.sync.dma_start(out=words[:], in_=tab_words[a].rearrange("p t i -> p (t i)").bitcast(I32))
             return words
 
@@ -112,36 +112,34 @@ def tile_list_approach_cue_scores_kernel(
             return tile
 
         nc.sync.dma_start(list1[:], offs)
-        for a in range(K_PASSES):
-            raw = load_w1(0, a)
-            words = load_table(a)
-            quantise_w1(0, a, round_w1(0, a, raw))
-            if a < K_PASSES - 1:
-                nc.vector.tensor_copy(v_words[a][:], words[:].bitcast(U32).indirect(list1[:]))
-                if a == 1:
-                    v_planes = placed("v_planes", [P, S], U8, TABLE_AT)
-                    nc.vector.tensor_copy(v_planes[:], tab_planes[:].indirect(list1[:]))
-            else:
-                for half in range(S // BANK):
-                    cols = slice(half * BANK, (half + 1) * BANK)
-                    part = list1[:, half * BANK // LIST_COLS : (half + 1) * BANK // LIST_COLS]
-                    nc.vector.tensor_copy(v_words[a][:, cols], words[:].bitcast(U32).indirect(part))
+        raws, tabs = {}, {}
+        raws[0], tabs[0], raws[1], raws[2] = load_w1(0, 0), load_table(0), load_w1(0, 1), load_w1(0, 2)
+        tabs[1], tabs[2] = load_table(1), load_table(2)
+        quantise_w1(0, 0, round_w1(0, 0, raws[0]))
+        nc.vector.tensor_copy(v_words[0][:], tabs[0][:].bitcast(U32).indirect(list1[:]))
+        v_planes = placed("v_planes", [P, S], U8, TABLE_AT)
+        nc.vector.tensor_copy(v_planes[:], tab_planes[:].indirect(list1[:]))
+        for a in range(1, K_PASSES):
+            quantise_w1(0, a, round_w1(0, a, raws[a]))
+        nc.vector.tensor_copy(v_words[1][:], tabs[1][:].bitcast(U32).indirect(list1[:]))
+        for half in range(S // BANK):
+            cols = slice(half * BANK, (half + 1) * BANK)
+            part = list1[:, half * BANK // LIST_COLS : (half + 1) * BANK // LIST_COLS]
+            nc.vector.tensor_copy(v_words[2][:, cols], tabs[2][:].bitcast(U32).indirect(part))
 
         def load_wgs(t):
             tile = placed(f"wgs{t}", [P, S], F32, WGS_AT + 4 * t)
-            for q in range(4):
+            for q in (0, 2, 1, 3):
                 nc.sync.dma_start(out=tile[32 * q : 32 * q + 32, :], in_=wgs_rows[:, t, :])
             return tile
 
-        motions, wgs_of, pages, raws = {}, {}, {}, {}
+        motions, wgs_of, pages = {}, {}, {}
         motions[0], wgs_of[0] = load_motion(0), load_wgs(0)
         nc.sync.dma_start(list2[:], offs2)
         pages[0] = load_page(0)
         motions[1], wgs_of[1], pages[1] = load_motion(1), load_wgs(1), load_page(1)
         motions[2], wgs_of[2], raws[0], pages[2] = load_motion(2), load_wgs(2), load_w1(1, 0), load_page(2)
-        raws[1], motions[3], wgs_of[3], raws[2] = load_w1(1, 1), load_motion(3), load_wgs(3), load_w1(1, 2)
-        nc.sync.dma_start(list3[:], offs3)
-        nc.sync.dma_start(out=wgt_sb[:], in_=wgt)
+        raws[1], raws[2], motions[3], wgs_of[3] = load_w1(1, 1), load_w1(1, 2), load_motion(3), load_wgs(3)
         pages[3] = load_page(3)
 
         def features(s):
@@ -177,10 +175,7 @@ def tile_list_approach_cue_scores_kernel(
 
         def round_x(name, picked, width, kib):
             rounded = placed(name, [P, width, PACK], BF16, kib)
-            nc.scalar.copy(
-                out=rounded[:].rearrange("p (c e) t -> p c t e", e=4),
-                in_=picked[:].rearrange("p t (c e) -> p c t e", e=4),
-            )
+            nc.scalar.copy(out=rounded[:], in_=picked[:].rearrange("p t m -> p m t"))
             return rounded
 
         def quantise_x(b, rounded, cols):
@@ -199,6 +194,9 @@ def tile_list_approach_cue_scores_kernel(
                 for later in range(PACK, SLICES):
                     motions[later] = load_motion(later)
                     pages[later] = load_page(later)
+                    if later == 5:
+                        nc.sync.dma_start(list3[:], offs3)
+                        nc.sync.dma_start(out=wgt_sb[:], in_=wgt)
                 nc.sync.dma_start(
                     out=w2_codes[:].bitcast(I32), in_=w2_words.rearrange("a p c -> p a c").bitcast(I32)
                 )
@@ -213,10 +211,10 @@ def tile_list_approach_cue_scores_kernel(
                     nc.sync.dma_start(out=tile[:], in_=vis_rows[:, 2 * pair : 2 * pair + 2, :])
                     vis_sb.append(tile)
             hs[s] = features(s)
-            if s == 0:
+            if s % PACK == 0:
                 for half in range(S // BANK):
                     cols = slice(half * BANK, (half + 1) * BANK)
-                    times_factors(nc.vector, s, hs[s], cols)
+                    times_factors(nc.vector if s == 0 else nc.gpsimd, s, hs[s], cols)
                     put(s, hs[s], cols)
             else:
                 times_factors(nc.gpsimd, s, hs[s], whole)

from contextlib import ExitStack

import concourse.mybir as mybir

K, H, N, T, S, T2, M = 1536, 1024, 768, 4096, 1024, 2048, 1024
FLOPS = 2 * K * H * S + 2 * H * N * M

F32 = mybir.dt.float32
BF16 = mybir.dt.bfloat16
I32 = mybir.dt.int32
U32 = mybir.dt.uint32
U16 = mybir.dt.uint16
U8 = mybir.dt.uint8
FP8X4 = mybir.dt.float8_e4m3fn_x4
FP4X4 = mybir.dt.float4_e2m1fn_x4
MULT = mybir.AluOpType.mult
TANH = mybir.ActivationFunctionType.Tanh

P = 128
PACK = 4
PASS = P * PACK
BANK = 512
K_PASSES = K // PASS
R_PASSES = H // PASS
SLICES = R_PASSES * PACK
LIST_COLS = 16
CUES = 256
KB = 1024


def tile_list_approach_cue_scores_kernel(
    tc, tab_words, tab_scales, offs, w1, b1, motion, page0, wgs, offs2, wgt, offs3, w2_words, w2_scales, vis, out
):
    nc = tc.nc
    with ExitStack() as ctx:
        keep = ctx.enter_context(tc.tile_pool(name="keep", bufs=1))
        arena = ctx.enter_context(tc.tile_pool(name="arena", bufs=1))
        psum = ctx.enter_context(tc.psum_pool(name="psum", bufs=4))

        def held(name, shape, dtype):
            return keep.tile(shape, dtype, name=name, align_bytes=64)

        def placed(name, shape, dtype, kib):
            return arena.tile(shape, dtype, name=name, align_bytes=64, offset=kib * KB)

        TABLE_AT, PAGES_AT, RAW_AT, ROUND_AT, MOTION_AT, H_AT, WGS_AT = 0, 49, 81, 105, 121, 137, 153

        list1 = held("list1", [P, S // LIST_COLS], U16)
        list2 = held("list2", [P, S // LIST_COLS], U16)
        list3 = held("list3", [P, M // LIST_COLS], U16)
        tab_planes = held("tab_planes", [P, T], U8)
        v_words = [held(f"v_words{a}", [P, S], U32) for a in range(K_PASSES)]
        w1_words = [[held(f"w1_words{b}_{a}", [P, PASS], U32) for a in range(K_PASSES)] for b in range(R_PASSES)]
        w1_plane = [[held(f"w1_plane{b}_{a}", [P, PASS], U8) for a in range(K_PASSES)] for b in range(R_PASSES)]
        bias = held("bias", [P, R_PASSES, PACK], F32)
        wgt_sb = held("wgt_sb", [P, M], F32)
        w2_codes = held("w2_codes", [P, R_PASSES, 2 * N], U8)
        w2_plane = held("w2_plane", [P, R_PASSES, N], U8)
        x_words = [held(f"x_words{b}", [P, M], U32) for b in range(R_PASSES)]
        x_plane = [held(f"x_plane{b}", [P, M], U8) for b in range(R_PASSES)]

        motion_rows = motion.rearrange("(b p t) j -> b t p j", b=R_PASSES, t=PACK)
        page_rows = page0.rearrange("(b p t) c -> b t p c", b=R_PASSES, t=PACK)
        wgs_rows = wgs.rearrange("(q t) j -> q t j", t=PACK)
        out_rows = out.rearrange("(i p) m -> p i m", p=P)
        vis_rows = vis.rearrange("(i p) m -> p i m", p=P)

        nc.gpsimd.memset(tab_planes[:].bitcast(U32), 0)
        for q in range(4):
            nc.gpsimd.dma_start(
                out=tab_planes[32 * q : 32 * q + 4 * K_PASSES, :].bitcast(I32),
                in_=tab_scales[:, 4 * q : 4 * q + 4, :].bitcast(I32),
            )
        nc.scalar.dma_start(out=bias[:], in_=b1.rearrange("(b p t) -> p b t", b=R_PASSES, t=PACK))
        nc.vector.memset(w2_plane[:].rearrange("p a c -> p (a c)").bitcast(U32), 0)

        def load_w1(b, a):
            raw = placed(f"w1_raw{b}_{a}", [P, PACK, PASS], F32, RAW_AT + 8 * a)
            rows = w1[a * PASS : (a + 1) * PASS, b * PASS : (b + 1) * PASS]
            nc.sync.dma_start(out=raw[:], in_=rows.rearrange("(p i) c -> p i c", i=PACK))
            return raw

        def round_w1(b, a, raw):
            rounded = placed(f"w1_round{b}_{a}", [P, PACK, P, PACK], BF16, ROUND_AT + 4 * ((b * K_PASSES + a) % 2))
            nc.scalar.copy(
                out=rounded[:].rearrange("p t q i -> p q t i"),
                in_=raw[:].rearrange("p i (q t) -> p q t i", t=PACK),
            )
            return rounded

        def quantise_w1(b, a, rounded):
            nc.vector.quantize_mx(
                out=w1_words[b][a][:].bitcast(FP8X4),
                scales=w1_plane[b][a][:],
                in_=rounded[:].rearrange("p t q i -> p (t q i)"),
            )

        def load_table(a):
            words = placed(f"tab{a}", [P, T], I32, TABLE_AT + 16 * a)
            nc.sync.dma_start(out=words[:], in_=tab_words[a].rearrange("p t i -> p (t i)").bitcast(I32))
            return words

        def load_motion(s):
            tile = placed(f"motion{s}", [P, S], F32, MOTION_AT + 4 * (s % 4))
            nc.sync.dma_start(out=tile[:], in_=motion_rows[s // PACK, s % PACK])
            return tile

        def load_page(s):
            at = PAGES_AT + 8 * s if s < PACK else TABLE_AT + 1 + 8 * (s - PACK)
            tile = placed(f"page{s}", [P, T2], F32, at)
            nc.sync.dma_start(out=tile[:], in_=page_rows[s // PACK, s % PACK])
            return tile

        nc.sync.dma_start(list1[:], offs)
        raws, tabs = {}, {}
        raws[0], tabs[0], raws[1], raws[2] = load_w1(0, 0), load_table(0), load_w1(0, 1), load_w1(0, 2)
        tabs[1], tabs[2] = load_table(1), load_table(2)
        quantise_w1(0, 0, round_w1(0, 0, raws[0]))
        nc.vector.tensor_copy(v_words[0][:], tabs[0][:].bitcast(U32).indirect(list1[:]))
        v_planes = placed("v_planes", [P, S], U8, TABLE_AT)
        nc.vector.tensor_copy(v_planes[:], tab_planes[:].indirect(list1[:]))
        for a in range(1, K_PASSES):
            quantise_w1(0, a, round_w1(0, a, raws[a]))
        nc.vector.tensor_copy(v_words[1][:], tabs[1][:].bitcast(U32).indirect(list1[:]))
        for half in range(S // BANK):
            cols = slice(half * BANK, (half + 1) * BANK)
            part = list1[:, half * BANK // LIST_COLS : (half + 1) * BANK // LIST_COLS]
            nc.vector.tensor_copy(v_words[2][:, cols], tabs[2][:].bitcast(U32).indirect(part))

        def load_wgs(t):
            tile = placed(f"wgs{t}", [P, S], F32, WGS_AT + 4 * t)
            for q in (0, 2, 1, 3):
                nc.sync.dma_start(out=tile[32 * q : 32 * q + 32, :], in_=wgs_rows[:, t, :])
            return tile

        motions, wgs_of, pages = {}, {}, {}
        motions[0], wgs_of[0] = load_motion(0), load_wgs(0)
        nc.sync.dma_start(list2[:], offs2)
        pages[0] = load_page(0)
        motions[1], wgs_of[1], pages[1] = load_motion(1), load_wgs(1), load_page(1)
        motions[2], wgs_of[2], raws[0], pages[2] = load_motion(2), load_wgs(2), load_w1(1, 0), load_page(2)
        raws[1], raws[2], motions[3], wgs_of[3] = load_w1(1, 1), load_w1(1, 2), load_motion(3), load_wgs(3)
        pages[3] = load_page(3)

        def features(s):
            b, t = divmod(s, PACK)
            h = placed(f"h{s}", [P, S], F32, TABLE_AT + 33 if s == 5 else H_AT + 4 * (s % 4))
            for half in range(S // BANK):
                cols = slice(half * BANK, (half + 1) * BANK)
                acc = psum.tile([P, BANK], F32, name="acc1")
                for a in range(K_PASSES):
                    nc.tensor.matmul_mx(
                        out=acc[:],
                        lhsT=w1_words[b][a][:, t * P : (t + 1) * P].bitcast(FP8X4),
                        lhsT_scale=w1_plane[b][a][:, t * P : (t + 1) * P],
                        rhs=v_words[a][:, cols].bitcast(FP8X4),
                        rhs_scale=v_planes[4 * a : P, cols],
                        start=(a == 0),
                        stop=(a == K_PASSES - 1),
                    )
                nc.scalar.activation(out=h[:, cols], in_=acc[:], func=TANH, bias=bias[:, b, t : t + 1])
            return h

        def times_factors(engine, s, h, cols):
            engine.tensor_tensor(h[:, cols], h[:, cols], motions[s][:, cols], MULT)
            engine.tensor_tensor(h[:, cols], h[:, cols], wgs_of[s % PACK][:, cols], MULT)

        def put(s, h, cols):
            part = list2[:, cols.start // LIST_COLS : cols.stop // LIST_COLS]
            nc.vector.tensor_copy(pages[s][:].indirect(part), h[:, cols])

        def pick(s, picked, cols):
            part = list3[:, cols.start // LIST_COLS : cols.stop // LIST_COLS]
            nc.vector.tensor_tensor(picked[:, s % PACK, :], pages[s][:].indirect(part), wgt_sb[:, cols], MULT)

        def round_x(name, picked, width, kib):
            rounded = placed(name, [P, width, PACK], BF16, kib)
            nc.scalar.copy(out=rounded[:], in_=picked[:].rearrange("p t m -> p m t"))
            return rounded

        def quantise_x(b, rounded, cols):
            nc.vector.quantize_mx(
                out=x_words[b][:, cols].bitcast(FP8X4),
                scales=x_plane[b][:, cols],
                in_=rounded[:].rearrange("p m t -> p (m t)"),
            )

        whole = slice(0, S)
        hs = {}
        for s in range(SLICES):
            if s == PACK - 1:
                for a in range(K_PASSES):
                    quantise_w1(1, a, round_w1(1, a, raws[a]))
                for later in range(PACK, SLICES):
                    motions[later] = load_motion(later)
                    pages[later] = load_page(later)
                    if later == 5:
                        nc.sync.dma_start(list3[:], offs3)
                        nc.sync.dma_start(out=wgt_sb[:], in_=wgt)
                nc.sync.dma_start(
                    out=w2_codes[:].bitcast(I32), in_=w2_words.rearrange("a p c -> p a c").bitcast(I32)
                )
                for q in range(4):
                    nc.sync.dma_start(
                        out=w2_plane[32 * q : 32 * q + 4, :, :].bitcast(I32),
                        in_=w2_scales[:, 4 * q : 4 * q + 4, :].rearrange("a r c -> r a c").bitcast(I32),
                    )
                vis_sb = []
                for pair in range(N // (2 * P)):
                    tile = placed(f"vis{pair}", [P, 2, M], F32, RAW_AT + 8 * pair)
                    nc.sync.dma_start(out=tile[:], in_=vis_rows[:, 2 * pair : 2 * pair + 2, :])
                    vis_sb.append(tile)
            hs[s] = features(s)
            if s % PACK == 0:
                for half in range(S // BANK):
                    cols = slice(half * BANK, (half + 1) * BANK)
                    times_factors(nc.vector if s == 0 else nc.gpsimd, s, hs[s], cols)
                    put(s, hs[s], cols)
            else:
                times_factors(nc.gpsimd, s, hs[s], whole)
                put(s, hs[s], whole)
            if s == 5:
                picked0 = placed("picked0", [P, PACK, M], F32, TABLE_AT + 33)
                for early in range(PACK):
                    pick(early, picked0, whole)
                quantise_x(0, round_x("x_round0", picked0, M, ROUND_AT + 8), whole)

        chunks = M // CUES
        picked_at = [TABLE_AT + 33, H_AT + 12, ROUND_AT, ROUND_AT + 4]
        round_at = [ROUND_AT, ROUND_AT + 4, ROUND_AT + 8, ROUND_AT + 10]

        def pick_chunk(c):
            cols = slice(c * CUES, (c + 1) * CUES)
            picked = placed(f"picked1_{c}", [P, PACK, CUES], F32, picked_at[c])
            for s in range(PACK, SLICES):
                pick(s, picked, cols)
            return round_x(f"x_round1_{c}", picked, CUES, round_at[c])

        def scores(c):
            cols = slice(c * CUES, (c + 1) * CUES)
            for pair in range(N // (2 * P)):
                acc = psum.tile([P, 2, CUES], F32, name="acc2")
                for u in range(2):
                    i = 2 * pair + u
                    for b in range(R_PASSES):
                        nc.tensor.matmul_mx(
                            out=acc[:, u, :],
                            lhsT=w2_codes[:, b, 2 * P * i : 2 * P * (i + 1)].bitcast(FP4X4),
                            lhsT_scale=w2_plane[:, b, P * i : P * (i + 1)],
                            rhs=x_words[b][:, cols].bitcast(FP8X4),
                            rhs_scale=x_plane[b][:, cols],
                            start=(b == 0),
                            stop=(b == R_PASSES - 1),
                        )
                y = placed(f"y{c}_{pair}", [P, 2, CUES], F32, PAGES_AT + 2 * (3 * c + pair))
                nc.scalar.activation(out=y[:], in_=acc[:], func=TANH)
                nc.vector.tensor_tensor(y[:], y[:], vis_sb[pair][:, :, cols], MULT)
                nc.sync.dma_start(out=out_rows[:, 2 * pair : 2 * pair + 2, cols], in_=y[:])

        rounded = {0: pick_chunk(0)}
        for c in range(chunks):
            if c + 1 < chunks:
                rounded[c + 1] = pick_chunk(c + 1)
            quantise_x(1, rounded[c], slice(c * CUES, (c + 1) * CUES))
        for c in range(chunks):
            scores(c)
